import numpy as np
import ml_dtypes


def mxq(x, axis, fmt="e4m3"):
    dtype, down = {"e4m3": (ml_dtypes.float8_e4m3fn, 7), "e5m2": (ml_dtypes.float8_e5m2, 14)}[fmt]
    v = np.moveaxis(np.asarray(x, np.float32).astype(ml_dtypes.bfloat16).astype(np.float64), axis, -1)
    blocks = v.reshape(v.shape[:-1] + (-1, 32))
    amax = np.abs(blocks).max(-1, keepdims=True)
    byte = np.maximum(np.where(amax > 0, np.frexp(amax)[1] - 1 + 127, 0) - down, 1)
    scale = np.exp2(byte - 127.0)
    codes = (blocks / scale).astype(np.float32).astype(dtype).astype(np.float64)
    return np.moveaxis((codes * scale).reshape(v.shape), -1, axis)


WIDE = False


def mx_kscale(k, group=512):
    if not WIDE:
        return np.ones(k)
    levels = np.array([18, -18])
    if group != 512:
        return np.exp2(np.random.permutation(np.resize(levels, k // group))).repeat(group)
    if k % 512:
        return np.exp2(np.random.permutation(np.resize(levels, k // 32))).repeat(32)
    a = np.empty((k // 512, 16))
    for p in range(k // 512):
        a[p, :8] = np.random.permutation(np.resize(levels, 8))
        for g in range(8):
            far = levels[np.abs(levels - a[p, g]) >= 10]
            a[p, g + 8] = far[np.random.randint(len(far))]
    return np.exp2(a.ravel()).repeat(32)


def f64(x):
    return np.asarray(x).astype(np.float64)


G, D, I, Q, E = 8, 128, 128, 128, 128


def sgn(shape):
    return np.random.uniform(0.5, 2.0, shape) * np.where(np.random.standard_normal(shape) < 0, -1.0, 1.0)


def setup_inputs():
    n = np.random.standard_normal
    s_d = mx_kscale(D, 0)
    s_i = mx_kscale(I, 0)
    return {
        "kT": (n((G, D, I)) / np.sqrt(D) / s_d[:, None]).astype(np.float32),
        "qT": (n((G, D, Q)) * s_d[:, None]).astype(np.float32),
        "rk": (np.random.uniform(0.5, 2.0, (G, I, 1))).astype(np.float32),
        "t": (sgn((G, I, 1)) * s_i[:, None]).astype(np.float32),
        "v": ((n((G, I, E))) / s_i[:, None]).astype(np.float32),
        "r": (n((G, Q, E))).astype(np.float32),
    }


def reference(kT, qT, rk, t, v, r):
    kTq = mxq(f64(kT), 1, "e4m3")
    qTq = mxq(f64(qT), 1, "e4m3")
    z = kTq.transpose(0, 2, 1) @ qTq
    p = np.maximum(z * f64(rk), 0.0) * f64(t)
    pq = mxq(p, 1, "e4m3")
    vq = mxq(f64(v), 1, "e4m3")
    y = pq.transpose(0, 2, 1) @ vq
    o = y / 8.0 + f64(r)
    return o

@@ -1,0 +1,222 @@
+from contextlib import ExitStack
+
+import concourse.mybir as mybir
+
+G, D, I, Q, E = 8, 128, 128, 128, 128
+FLOPS = 2 * G * I * Q * (D + E)
+
+F32 = mybir.dt.float32
+BF16 = mybir.dt.bfloat16
+U32 = mybir.dt.uint32
+U8 = mybir.dt.uint8
+FP8X4 = mybir.dt.float8_e4m3fn_x4
+ALU = mybir.AluOpType
+ACT = mybir.ActivationFunctionType
+
+P = 128
+ROWS = 32
+TILES = 4
+SETS = 2
+PACK = 4
+W = 128
+K_AT = 128
+Q_AT = 256
+KQ_WIDTH = 384
+
+
+def tile_rows_win_cos_res_kernel(tc, kT, qT, rk, t, v, r, out):
+    nc = tc.nc
+    with ExitStack() as ctx:
+        sb = ctx.enter_context(tc.tile_pool(name="sb", bufs=1))
+        ps = ctx.enter_context(tc.psum_pool(name="ps", bufs=1))
+        ctx.enter_context(tc.manual_schedule())
+
+        def sets(name, shape, dtype):
+            return [sb.tile(shape, dtype, name="%s%d" % (name, h), align_bytes=64) for h in range(SETS)]
+
+        k_raw = sets("k_raw", [P, PACK, W], F32)
+        q_raw = sets("q_raw", [P, PACK, W], F32)
+        v_raw = sb.tile([P, SETS, PACK, W], F32, name="v_raw")
+        r_sb = sb.tile([P, G, W], F32, name="r_sb")
+        rk_sb = sb.tile([P, SETS, 8], F32, name="rk_sb")
+        t_sb = sb.tile([P, SETS, 8], F32, name="t_sb")
+        warm = sb.tile([P, 8], F32, name="warm")
+        warm_out = sb.tile([P, 8], F32, name="warm_out")
+        k_bf = sets("k_bf", [P, W * PACK], BF16)
+        q_bf = sets("q_bf", [P, W * PACK], BF16)
+        v_bf = sets("v_bf", [P, W * PACK], BF16)
+        p_bf = sets("p_bf", [P, W * PACK], BF16)
+        kq_codes = sets("kq_codes", [P, KQ_WIDTH], U32)
+        kq_scales = sets("kq_scales", [P, KQ_WIDTH], U8)
+        k_shifted = sets("k_shifted", [P, KQ_WIDTH], U8)
+        v_codes = sets("v_codes", [P, W], U32)
+        v_scales = sets("v_scales", [P, W], U8)
+        p_codes = sets("p_codes", [P, W], U32)
+        p_scales = sets("p_scales", [P, W], U8)
+        clipped = sets("clipped", [P, PACK, W], F32)
+        o_sb = sets("o_sb", [P, TILES, W], F32)
+        banks = [[ps.tile([P, PACK, W], F32, name="bank%d_%d" % (h, g)) for g in range(TILES)] for h in range(SETS)]
+
+        def rows(g):
+            return slice(ROWS * g, ROWS * (g + 1))
+
+        def windows(x, h):
+            return x[TILES * h : TILES * (h + 1)].rearrange("g (p j) c -> (g p) j c", j=PACK)
+
+        for h in range(SETS):
+            nc.sync.dma_start(out=k_raw[h][:], in_=windows(kT, h))
+            nc.sync.dma_start(out=q_raw[h][:], in_=windows(qT, h))
+        nc.scalar.dma_start(out=rk_sb[:, :, 0:PACK], in_=rk.rearrange("(h g) (p j) o -> (g p) h (j o)", h=SETS, j=PACK))
+        nc.scalar.dma_start(out=t_sb[:, :, 0:PACK], in_=t.rearrange("(h g) (p j) o -> (g p) h (j o)", h=SETS, j=PACK))
+        nc.sync.dma_start(out=v_raw[:], in_=v.rearrange("(h g) (p j) e -> (g p) h j e", h=SETS, j=PACK))
+        nc.sync.dma_start(out=r_sb[:], in_=r.rearrange("g q e -> q g e"))
+
+        nc.vector.memset(warm[:], 0.0)
+        nc.scalar.activation(out=warm_out[:], in_=warm[:], func=ACT.Relu)
+        for h in range(SETS):
+            nc.vector.memset(kq_codes[h][:, 0:K_AT], 0)
+            nc.vector.memset(kq_scales[h][:].bitcast(U32), 0)
+            nc.vector.memset(k_shifted[h][:].bitcast(U32), 0)
+
+        def cast(eng, dst, src):
+            if eng == "v":
+                nc.vector.tensor_copy(out=dst, in_=src)
+            else:
+                nc.scalar.copy(out=dst, in_=src)
+
+        def cast_k(h, eng):
+            cast(eng, k_bf[h][:].rearrange("p (c s j) -> p s j c", c=PACK, j=PACK), k_raw[h][:].rearrange("p j (s c) -> p s j c", c=PACK))
+
+        def cast_plain(eng, dst, src):
+            cast(eng, dst.rearrange("p (c i j) -> p c j i", i=4, j=PACK), src.rearrange("p j (c i) -> p c j i", i=4))
+
+        def cast_q(h, eng):
+            cast_plain(eng, q_bf[h][:], q_raw[h][:])
+
+        def cast_v(h, eng):
+            cast_plain(eng, v_bf[h][:], v_raw[:, h])
+
+        def quant(codes, scales, src):
+            nc.vector.quantize_mx(out=codes.bitcast(FP8X4), scales=scales, in_=src)
+
+        def quant_k(h):
+            quant(kq_codes[h][:, K_AT : K_AT + W], kq_scales[h][:, K_AT : K_AT + W], k_bf[h][:])
+
+        def quant_q(h):
+            quant(kq_codes[h][:, Q_AT : Q_AT + W], kq_scales[h][:, Q_AT : Q_AT + W], q_bf[h][:])
+
+        def quant_v(h):
+            quant(v_codes[h][:], v_scales[h][:], v_bf[h][:])
+
+        def quant_p(h):
+            quant(p_codes[h][:], p_scales[h][:], p_bf[h][:])
+
+        def shift_scales(h):
+            nc.vector.tensor_copy(out=k_shifted[h][:, K_AT + ROWS : K_AT + ROWS + W], in_=kq_scales[h][:, K_AT : K_AT + W])
+
+        def scores(h):
+            for first, c, g2 in [(a, b, d) for a in range(2) for b in range(PACK) for d in range(2)]:
+                for g in (first + 2 * g2,):
+                    at = K_AT + ROWS * (c - g)
+                    if (c - g) % 2 == 0:
+                        k_scale = kq_scales[h][rows(g), at : at + W]
+                    else:
+                        k_scale = k_shifted[h][rows(g), at + ROWS : at + ROWS + W]
+                    nc.tensor.matmul_mx(
+                        out=banks[h][g][:, c, :],
+                        lhsT=kq_codes[h][rows(g), at : at + W].bitcast(FP8X4),
+                        lhsT_scale=k_scale,
+                        rhs=kq_codes[h][rows(g), Q_AT : Q_AT + W].bitcast(FP8X4),
+                        rhs_scale=kq_scales[h][rows(g), Q_AT : Q_AT + W],
+                        start=True,
+                        stop=True,
+                    )
+
+        def clip(h, g, eng):
+            if eng == "s":
+                for c in range(PACK):
+                    nc.scalar.activation(out=clipped[h][rows(g), c, :], in_=banks[h][g][rows(g), c, :], func=ACT.Relu, scale=rk_sb[rows(g), h, c : c + 1])
+            else:
+                nc.vector.tensor_tensor(
+                    out=clipped[h][rows(g)],
+                    in0=banks[h][g][rows(g)],
+                    in1=rk_sb[rows(g), h, 0:PACK].unsqueeze(2).to_broadcast([ROWS, PACK, W]),
+                    op=ALU.mult,
+                )
+
+        def weights(h):
+            nc.vector.scalar_tensor_tensor(
+                out=p_bf[h][:].rearrange("p (q c) -> p q c", c=PACK),
+                in0=clipped[h][:].rearrange("p c q -> p q c"),
+                scalar=0.0,
+                in1=t_sb[:, h, 0:PACK].unsqueeze(1).to_broadcast([P, W, PACK]),
+                op0=ALU.max,
+                op1=ALU.mult,
+            )
+
+        def values(h):
+            for g in range(TILES):
+                nc.tensor.matmul_mx(
+                    out=banks[h][g][:, 0, :],
+                    lhsT=p_codes[h][rows(g), :].bitcast(FP8X4),
+                    lhsT_scale=p_scales[h][rows(g), :],
+                    rhs=v_codes[h][rows(g), :].bitcast(FP8X4),
+                    rhs_scale=v_scales[h][rows(g), :],
+                    start=True,
+                    stop=True,
+                )
+
+        def finish(h, g):
+            nc.vector.scalar_tensor_tensor(
+                out=o_sb[h][:, g, :],
+                in0=banks[h][g][:, 0, :],
+                scalar=0.125,
+                in1=r_sb[:, TILES * h + g, :],
+                op0=ALU.mult,
+                op1=ALU.add,
+            )
+
+        def store(queue, h, g0, g1):
+            queue.dma_start(out=out[TILES * h + g0 : TILES * h + g1].rearrange("g q e -> q g e"), in_=o_sb[h][:, g0:g1, :])
+
+        cast_k(0, "s")
+        cast_q(0, "v")
+        quant_k(0)
+        quant_q(0)
+        shift_scales(0)
+        scores(0)
+        cast_k(1, "s")
+        cast_q(1, "v")
+        quant_k(1)
+        quant_q(1)
+        shift_scales(1)
+        scores(1)
+        clip(0, 0, "s")
+        clip(0, 1, "s")
+        clip(0, 2, "v")
+        clip(0, 3, "v")
+        clip(1, 3, "v")
+        clip(1, 0, "s")
+        clip(1, 1, "s")
+        clip(1, 2, "s")
+        weights(0)
+        cast_v(0, "v")
+        cast_v(1, "s")
+        quant_p(0)
+        weights(1)
+        quant_v(0)
+        values(0)
+        quant_p(1)
+        quant_v(1)
+        values(1)
+        finish(0, 0)
+        finish(0, 1)
+        finish(0, 2)
+        finish(0, 3)
+        store(nc.sync, 0, 0, 4)
+        finish(1, 0)
+        finish(1, 1)
+        store(nc.sync, 1, 0, 2)
+        finish(1, 2)
+        finish(1, 3)
+        store(nc.scalar, 1, 2, 4)

@@ -22,6 +22,7 @@ W = 128
 K_AT = 128
 Q_AT = 256
 KQ_WIDTH = 384
+Q_SPLIT = 80
 
 
 def tile_rows_win_cos_res_kernel(tc, kT, qT, rk, t, v, r, out):
@@ -37,7 +38,7 @@ def tile_rows_win_cos_res_kernel(tc, kT, qT, rk, t, v, r, out):
         k_raw = sets("k_raw", [P, PACK, W], F32)
         q_raw = sets("q_raw", [P, PACK, W], F32)
         v_raw = sb.tile([P, SETS, PACK, W], F32, name="v_raw")
-        r_sb = sb.tile([P, G, W], F32, name="r_sb")
+        r_sb = sets("r_sb", [P, TILES, W], F32)
         rk_sb = sb.tile([P, SETS, 8], F32, name="rk_sb")
         t_sb = sb.tile([P, SETS, 8], F32, name="t_sb")
         warm = sb.tile([P, 8], F32, name="warm")
@@ -67,9 +68,10 @@ def tile_rows_win_cos_res_kernel(tc, kT, qT, rk, t, v, r, out):
             nc.sync.dma_start(out=k_raw[h][:], in_=windows(kT, h))
             nc.sync.dma_start(out=q_raw[h][:], in_=windows(qT, h))
         nc.scalar.dma_start(out=rk_sb[:, :, 0:PACK], in_=rk.rearrange("(h g) (p j) o -> (g p) h (j o)", h=SETS, j=PACK))
-        nc.scalar.dma_start(out=t_sb[:, :, 0:PACK], in_=t.rearrange("(h g) (p j) o -> (g p) h (j o)", h=SETS, j=PACK))
         nc.sync.dma_start(out=v_raw[:], in_=v.rearrange("(h g) (p j) e -> (g p) h j e", h=SETS, j=PACK))
-        nc.sync.dma_start(out=r_sb[:], in_=r.rearrange("g q e -> q g e"))
+        nc.sync.dma_start(out=t_sb[:, :, 0:PACK], in_=t.rearrange("(h g) (p j) o -> (g p) h (j o)", h=SETS, j=PACK))
+        for h in range(SETS):
+            nc.sync.dma_start(out=r_sb[h][:], in_=r[TILES * h : TILES * (h + 1)].rearrange("g q e -> q g e"))
 
         nc.vector.memset(warm[:], 0.0)
         nc.scalar.activation(out=warm_out[:], in_=warm[:], func=ACT.Relu)
@@ -81,6 +83,8 @@ def tile_rows_win_cos_res_kernel(tc, kT, qT, rk, t, v, r, out):
         def cast(eng, dst, src):
             if eng == "v":
                 nc.vector.tensor_copy(out=dst, in_=src)
+            elif eng == "g":
+                nc.gpsimd.tensor_scalar(out=dst, in0=src, scalar1=1.0, scalar2=0.0, op0=ALU.mult, op1=ALU.add)
             else:
                 nc.scalar.copy(out=dst, in_=src)
 
@@ -93,8 +97,15 @@ def tile_rows_win_cos_res_kernel(tc, kT, qT, rk, t, v, r, out):
         def cast_q(h, eng):
             cast_plain(eng, q_bf[h][:], q_raw[h][:])
 
+        def cast_q_shared(h):
+            cast_plain("s", q_bf[h][:, PACK * Q_SPLIT :], q_raw[h][:, :, Q_SPLIT:])
+            cast_plain("v", q_bf[h][:, : PACK * Q_SPLIT], q_raw[h][:, :, :Q_SPLIT])
+
         def cast_v(h, eng):
-            cast_plain(eng, v_bf[h][:], v_raw[:, h])
+            if eng == "g":
+                cast(eng, v_bf[h][:].rearrange("p (c j) -> p c j", j=PACK), v_raw[:, h].rearrange("p j c -> p c j"))
+            else:
+                cast_plain(eng, v_bf[h][:], v_raw[:, h])
 
         def quant(codes, scales, src):
             nc.vector.quantize_mx(out=codes.bitcast(FP8X4), scales=scales, in_=src)
@@ -114,9 +125,9 @@ def tile_rows_win_cos_res_kernel(tc, kT, qT, rk, t, v, r, out):
         def shift_scales(h):
             nc.vector.tensor_copy(out=k_shifted[h][:, K_AT + ROWS : K_AT + ROWS + W], in_=kq_scales[h][:, K_AT : K_AT + W])
 
-        def scores(h):
-            for first, c, g2 in [(a, b, d) for a in range(2) for b in range(PACK) for d in range(2)]:
-                for g in (first + 2 * g2,):
+        def scores(h, pair):
+            for c in range(PACK):
+                for g in pair:
                     at = K_AT + ROWS * (c - g)
                     if (c - g) % 2 == 0:
                         k_scale = kq_scales[h][rows(g), at : at + W]
@@ -171,7 +182,7 @@ def tile_rows_win_cos_res_kernel(tc, kT, qT, rk, t, v, r, out):
                 out=o_sb[h][:, g, :],
                 in0=banks[h][g][:, 0, :],
                 scalar=0.125,
-                in1=r_sb[:, TILES * h + g, :],
+                in1=r_sb[h][:, g, :],
                 op0=ALU.mult,
                 op1=ALU.add,
             )
@@ -180,34 +191,36 @@ def tile_rows_win_cos_res_kernel(tc, kT, qT, rk, t, v, r, out):
             queue.dma_start(out=out[TILES * h + g0 : TILES * h + g1].rearrange("g q e -> q g e"), in_=o_sb[h][:, g0:g1, :])
 
         cast_k(0, "s")
-        cast_q(0, "v")
+        cast_q_shared(0)
         quant_k(0)
         quant_q(0)
         shift_scales(0)
-        scores(0)
+        scores(0, (0, 1))
+        scores(0, (2, 3))
         cast_k(1, "s")
-        cast_q(1, "v")
+        cast_q_shared(1)
         quant_k(1)
         quant_q(1)
         shift_scales(1)
-        scores(1)
-        clip(0, 0, "s")
+        scores(1, (0, 3))
+        scores(1, (1, 2))
+        clip(0, 0, "v")
         clip(0, 1, "s")
-        clip(0, 2, "v")
-        clip(0, 3, "v")
+        clip(0, 2, "s")
+        clip(0, 3, "s")
+        clip(1, 0, "v")
         clip(1, 3, "v")
-        clip(1, 0, "s")
         clip(1, 1, "s")
         clip(1, 2, "s")
+        cast_v(0, "g")
         weights(0)
-        cast_v(0, "v")
+        quant_v(0)
         cast_v(1, "s")
         quant_p(0)
-        weights(1)
-        quant_v(0)
         values(0)
-        quant_p(1)
+        weights(1)
         quant_v(1)
+        quant_p(1)
         values(1)
         finish(0, 0)
         finish(0, 1)

@@ -213,16 +213,16 @@ def tile_rows_win_cos_res_kernel(tc, kT, qT, rk, t, v, r, out):
         clip(1, 1, "s")
         clip(1, 2, "s")
         cast_v(0, "g")
+        cast_v(1, "g")
         weights(0)
         quant_v(0)
-        cast_v(1, "s")
         quant_p(0)
         values(0)
-        weights(1)
         quant_v(1)
+        weights(1)
+        finish(0, 0)
         quant_p(1)
         values(1)
-        finish(0, 0)
         finish(0, 1)
         finish(0, 2)
         finish(0, 3)

from contextlib import ExitStack

import concourse.mybir as mybir

G, D, I, Q, E = 8, 128, 128, 128, 128
FLOPS = 2 * G * I * Q * (D + E)

F32 = mybir.dt.float32
BF16 = mybir.dt.bfloat16
U32 = mybir.dt.uint32
U8 = mybir.dt.uint8
FP8X4 = mybir.dt.float8_e4m3fn_x4
ALU = mybir.AluOpType
ACT = mybir.ActivationFunctionType

P = 128
ROWS = 32
TILES = 4
SETS = 2
PACK = 4
W = 128
K_AT = 128
Q_AT = 256
KQ_WIDTH = 384
Q_SPLIT = 80


def tile_rows_win_cos_res_kernel(tc, kT, qT, rk, t, v, r, out):
    nc = tc.nc
    with ExitStack() as ctx:
        sb = ctx.enter_context(tc.tile_pool(name="sb", bufs=1))
        ps = ctx.enter_context(tc.psum_pool(name="ps", bufs=1))
        ctx.enter_context(tc.manual_schedule())

        def sets(name, shape, dtype):
            return [sb.tile(shape, dtype, name="%s%d" % (name, h), align_bytes=64) for h in range(SETS)]

        k_raw = sets("k_raw", [P, PACK, W], F32)
        q_raw = sets("q_raw", [P, PACK, W], F32)
        v_raw = sb.tile([P, SETS, PACK, W], F32, name="v_raw")
        r_sb = sets("r_sb", [P, TILES, W], F32)
        rk_sb = sb.tile([P, SETS, 8], F32, name="rk_sb")
        t_sb = sb.tile([P, SETS, 8], F32, name="t_sb")
        warm = sb.tile([P, 8], F32, name="warm")
        warm_out = sb.tile([P, 8], F32, name="warm_out")
        k_bf = sets("k_bf", [P, W * PACK], BF16)
        q_bf = sets("q_bf", [P, W * PACK], BF16)
        v_bf = sets("v_bf", [P, W * PACK], BF16)
        p_bf = sets("p_bf", [P, W * PACK], BF16)
        kq_codes = sets("kq_codes", [P, KQ_WIDTH], U32)
        kq_scales = sets("kq_scales", [P, KQ_WIDTH], U8)
        k_shifted = sets("k_shifted", [P, KQ_WIDTH], U8)
        v_codes = sets("v_codes", [P, W], U32)
        v_scales = sets("v_scales", [P, W], U8)
        p_codes = sets("p_codes", [P, W], U32)
        p_scales = sets("p_scales", [P, W], U8)
        clipped = sets("clipped", [P, PACK, W], F32)
        o_sb = sets("o_sb", [P, TILES, W], F32)
        banks = [[ps.tile([P, PACK, W], F32, name="bank%d_%d" % (h, g)) for g in range(TILES)] for h in range(SETS)]

        def rows(g):
            return slice(ROWS * g, ROWS * (g + 1))

        def windows(x, h):
            return x[TILES * h : TILES * (h + 1)].rearrange("g (p j) c -> (g p) j c", j=PACK)

        for h in range(SETS):
            nc.sync.dma_start(out=k_raw[h][:], in_=windows(kT, h))
            nc.sync.dma_start(out=q_raw[h][:], in_=windows(qT, h))
        nc.scalar.dma_start(out=rk_sb[:, :, 0:PACK], in_=rk.rearrange("(h g) (p j) o -> (g p) h (j o)", h=SETS, j=PACK))
        nc.sync.dma_start(out=v_raw[:], in_=v.rearrange("(h g) (p j) e -> (g p) h j e", h=SETS, j=PACK))
        nc.sync.dma_start(out=t_sb[:, :, 0:PACK], in_=t.rearrange("(h g) (p j) o -> (g p) h (j o)", h=SETS, j=PACK))
        for h in range(SETS):
            nc.sync.dma_start(out=r_sb[h][:], in_=r[TILES * h : TILES * (h + 1)].rearrange("g q e -> q g e"))

        nc.vector.memset(warm[:], 0.0)
        nc.scalar.activation(out=warm_out[:], in_=warm[:], func=ACT.Relu)
        for h in range(SETS):
            nc.vector.memset(kq_codes[h][:, 0:K_AT], 0)
            nc.vector.memset(kq_scales[h][:].bitcast(U32), 0)
            nc.vector.memset(k_shifted[h][:].bitcast(U32), 0)

        def cast(eng, dst, src):
            if eng == "v":
                nc.vector.tensor_copy(out=dst, in_=src)
            elif eng == "g":
                nc.gpsimd.tensor_scalar(out=dst, in0=src, scalar1=1.0, scalar2=0.0, op0=ALU.mult, op1=ALU.add)
            else:
                nc.scalar.copy(out=dst, in_=src)

        def cast_k(h, eng):
            cast(eng, k_bf[h][:].rearrange("p (c s j) -> p s j c", c=PACK, j=PACK), k_raw[h][:].rearrange("p j (s c) -> p s j c", c=PACK))

        def cast_plain(eng, dst, src):
            cast(eng, dst.rearrange("p (c i j) -> p c j i", i=4, j=PACK), src.rearrange("p j (c i) -> p c j i", i=4))

        def cast_q(h, eng):
            cast_plain(eng, q_bf[h][:], q_raw[h][:])

        def cast_q_shared(h):
            cast_plain("s", q_bf[h][:, PACK * Q_SPLIT :], q_raw[h][:, :, Q_SPLIT:])
            cast_plain("v", q_bf[h][:, : PACK * Q_SPLIT], q_raw[h][:, :, :Q_SPLIT])

        def cast_v(h, eng):
            if eng == "g":
                cast(eng, v_bf[h][:].rearrange("p (c j) -> p c j", j=PACK), v_raw[:, h].rearrange("p j c -> p c j"))
            else:
                cast_plain(eng, v_bf[h][:], v_raw[:, h])

        def quant(codes, scales, src):
            nc.vector.quantize_mx(out=codes.bitcast(FP8X4), scales=scales, in_=src)

        def quant_k(h):
            quant(kq_codes[h][:, K_AT : K_AT + W], kq_scales[h][:, K_AT : K_AT + W], k_bf[h][:])

        def quant_q(h):
            quant(kq_codes[h][:, Q_AT : Q_AT + W], kq_scales[h][:, Q_AT : Q_AT + W], q_bf[h][:])

        def quant_v(h):
            quant(v_codes[h][:], v_scales[h][:], v_bf[h][:])

        def quant_p(h):
            quant(p_codes[h][:], p_scales[h][:], p_bf[h][:])

        def shift_scales(h):
            nc.vector.tensor_copy(out=k_shifted[h][:, K_AT + ROWS : K_AT + ROWS + W], in_=kq_scales[h][:, K_AT : K_AT + W])

        def scores(h, pair):
            for c in range(PACK):
                for g in pair:
                    at = K_AT + ROWS * (c - g)
                    if (c - g) % 2 == 0:
                        k_scale = kq_scales[h][rows(g), at : at + W]
                    else:
                        k_scale = k_shifted[h][rows(g), at + ROWS : at + ROWS + W]
                    nc.tensor.matmul_mx(
                        out=banks[h][g][:, c, :],
                        lhsT=kq_codes[h][rows(g), at : at + W].bitcast(FP8X4),
                        lhsT_scale=k_scale,
                        rhs=kq_codes[h][rows(g), Q_AT : Q_AT + W].bitcast(FP8X4),
                        rhs_scale=kq_scales[h][rows(g), Q_AT : Q_AT + W],
                        start=True,
                        stop=True,
                    )

        def clip(h, g, eng):
            if eng == "s":
                for c in range(PACK):
                    nc.scalar.activation(out=clipped[h][rows(g), c, :], in_=banks[h][g][rows(g), c, :], func=ACT.Relu, scale=rk_sb[rows(g), h, c : c + 1])
            else:
                nc.vector.tensor_tensor(
                    out=clipped[h][rows(g)],
                    in0=banks[h][g][rows(g)],
                    in1=rk_sb[rows(g), h, 0:PACK].unsqueeze(2).to_broadcast([ROWS, PACK, W]),
                    op=ALU.mult,
                )

        def weights(h):
            nc.vector.scalar_tensor_tensor(
                out=p_bf[h][:].rearrange("p (q c) -> p q c", c=PACK),
                in0=clipped[h][:].rearrange("p c q -> p q c"),
                scalar=0.0,
                in1=t_sb[:, h, 0:PACK].unsqueeze(1).to_broadcast([P, W, PACK]),
                op0=ALU.max,
                op1=ALU.mult,
            )

        def values(h):
            for g in range(TILES):
                nc.tensor.matmul_mx(
                    out=banks[h][g][:, 0, :],
                    lhsT=p_codes[h][rows(g), :].bitcast(FP8X4),
                    lhsT_scale=p_scales[h][rows(g), :],
                    rhs=v_codes[h][rows(g), :].bitcast(FP8X4),
                    rhs_scale=v_scales[h][rows(g), :],
                    start=True,
                    stop=True,
                )

        def finish(h, g):
            nc.vector.scalar_tensor_tensor(
                out=o_sb[h][:, g, :],
                in0=banks[h][g][:, 0, :],
                scalar=0.125,
                in1=r_sb[h][:, g, :],
                op0=ALU.mult,
                op1=ALU.add,
            )

        def store(queue, h, g0, g1):
            queue.dma_start(out=out[TILES * h + g0 : TILES * h + g1].rearrange("g q e -> q g e"), in_=o_sb[h][:, g0:g1, :])

        cast_k(0, "s")
        cast_q_shared(0)
        quant_k(0)
        quant_q(0)
        shift_scales(0)
        scores(0, (0, 1))
        scores(0, (2, 3))
        cast_k(1, "s")
        cast_q_shared(1)
        quant_k(1)
        quant_q(1)
        shift_scales(1)
        scores(1, (0, 3))
        scores(1, (1, 2))
        clip(0, 0, "v")
        clip(0, 1, "s")
        clip(0, 2, "s")
        clip(0, 3, "s")
        clip(1, 0, "v")
        clip(1, 3, "v")
        clip(1, 1, "s")
        clip(1, 2, "s")
        cast_v(0, "g")
        cast_v(1, "g")
        weights(0)
        quant_v(0)
        quant_p(0)
        values(0)
        quant_v(1)
        weights(1)
        finish(0, 0)
        quant_p(1)
        values(1)
        finish(0, 1)
        finish(0, 2)
        finish(0, 3)
        store(nc.sync, 0, 0, 4)
        finish(1, 0)
        finish(1, 1)
        store(nc.sync, 1, 0, 2)
        finish(1, 2)
        finish(1, 3)
        store(nc.scalar, 1, 2, 4)
